import numpy as np
import ml_dtypes


def mxq(x, axis, fmt="e4m3"):
    dtype, down = {"e4m3": (ml_dtypes.float8_e4m3fn, 7), "e5m2": (ml_dtypes.float8_e5m2, 14)}[fmt]
    v = np.moveaxis(np.asarray(x, np.float32).astype(ml_dtypes.bfloat16).astype(np.float64), axis, -1)
    blocks = v.reshape(v.shape[:-1] + (-1, 32))
    amax = np.abs(blocks).max(-1, keepdims=True)
    byte = np.maximum(np.where(amax > 0, np.frexp(amax)[1] - 1 + 127, 0) - down, 1)
    scale = np.exp2(byte - 127.0)
    codes = (blocks / scale).astype(np.float32).astype(dtype).astype(np.float64)
    return np.moveaxis((codes * scale).reshape(v.shape), -1, axis)


WIDE = False


def mx_kscale(k):
    if not WIDE:
        return np.ones(k)
    levels = np.array([30, -30])
    if k % 512:
        return np.exp2(np.random.permutation(np.resize(levels, k // 32))).repeat(32)
    a = np.empty((k // 512, 16))
    for p in range(k // 512):
        a[p, :8] = np.random.permutation(np.resize(levels, 8))
        for g in range(8):
            far = levels[np.abs(levels - a[p, g]) >= 10]
            a[p, g + 8] = far[np.random.randint(len(far))]
    return np.exp2(a.ravel()).repeat(32)


def f64(x):
    return np.asarray(x).astype(np.float64)


def striped(idx):
    return np.tile(np.asarray(idx).reshape(-1, 16).T, (8, 1)).astype(np.uint16)


def unstriped(offs):
    return offs[:16].T.reshape(-1).astype(np.int64)


E2M1 = np.array([0.0, 0.5, 1.0, 1.5, 2.0, 3.0, 4.0, 6.0, -0.0, -0.5, -1.0, -1.5, -2.0, -3.0, -4.0, -6.0])


def pack_weight(w, fmt):
    k, n = w.shape
    w = f64(np.asarray(w, np.float32).astype(ml_dtypes.bfloat16)).reshape(k // 32, 32, n)
    amax = np.abs(w).max(1)
    if fmt in ("e4m3", "e5m2"):
        byte = np.frexp(amax)[1] - 1 + 127 - (7 if fmt == "e4m3" else 14)
    else:
        mant, ex = np.frexp(amax / 6.0)
        byte = np.where(mant > 0.5, ex, ex - 1) + 127
    byte = np.clip(np.where(amax > 0, byte, 1), 1, 254)
    scaled = (w * np.exp2(127.0 - byte)[:, None, :]).reshape(k, n).astype(np.float32)
    by_word = np.ascontiguousarray(scaled.reshape(k // 512, 128, 4, n).transpose(0, 1, 3, 2))
    if fmt in ("e4m3", "e5m2"):
        words = by_word.astype(ml_dtypes.float8_e4m3fn if fmt == "e4m3" else ml_dtypes.float8_e5m2).view(np.uint8)
    else:
        c = by_word.astype(ml_dtypes.float4_e2m1fn).view(np.uint8) & 0xF
        words = (c[..., 0::2] | (c[..., 1::2] << 4)).reshape(k // 512, 128, 2 * n)
    return np.ascontiguousarray(words), np.ascontiguousarray(byte.astype(np.uint8).reshape(k // 512, 16, n))


def unpack_weight(words, scales, fmt):
    g, _, n = scales.shape
    words = np.ascontiguousarray(words).reshape(g, 128, n, -1)
    if fmt in ("e4m3", "e5m2"):
        vals = words.view(ml_dtypes.float8_e4m3fn if fmt == "e4m3" else ml_dtypes.float8_e5m2).astype(np.float64)
    else:
        nib = np.empty((g, 128, n, 4), np.uint8)
        nib[..., 0::2] = words & 0xF
        nib[..., 1::2] = words >> 4
        vals = E2M1[nib]
    vals = vals * np.repeat(np.exp2(scales.astype(np.float64) - 127.0), 8, axis=1)[..., None]
    return vals.transpose(0, 1, 3, 2).reshape(g * 512, n)


K, T, J, I, R, C, Q = 512, 512, 256, 256, 512, 512, 512


def setup_inputs():
    n = np.random.standard_normal
    idx = np.random.permutation(T)[:J]
    idx2 = np.random.permutation(T)[:I]
    idx3 = np.random.permutation(C)[:I]
    idx4 = np.random.permutation(Q)[:I]
    fk = mx_kscale(K)
    fr = mx_kscale(R)
    xtp = pack_weight(n((K, T)) / fk[:, None], "e4m3")
    wap = pack_weight(n((K, R)) * 0.5 / np.sqrt(K) * fk[:, None] * fr, "e2m1")
    wbp = pack_weight(n((K, R)) * 1 / np.sqrt(K) * fk[:, None] / fr, "e5m2")
    return {
        "xt_words": xtp[0],
        "xt_scales": xtp[1],
        "wa_words": wap[0],
        "wa_scales": wap[1],
        "wb_words": wbp[0],
        "wb_scales": wbp[1],
        "tf": (n((R, C))).astype(np.float32),
        "tv": (1.0 * n((J, Q))).astype(np.float32),
        "offs": striped(idx),
        "offs2": striped(idx2),
        "offs3": striped(idx3),
        "offs4": striped(idx4),
    }


def reference(xt_words, xt_scales, wa_words, wa_scales, wb_words, wb_scales, tf, tv, offs, offs2, offs3, offs4):
    idx = unstriped(offs)
    idx2 = unstriped(offs2)
    idx3 = unstriped(offs3)
    idx4 = unstriped(offs4)
    xtu = unpack_weight(xt_words, xt_scales, "e4m3")
    wau = unpack_weight(wa_words, wa_scales, "e2m1")
    wbu = unpack_weight(wb_words, wb_scales, "e5m2")
    xtidxg = xtu[:, idx]
    za = wau.T @ xtidxg
    ya1 = np.pad(za, ((0, 0), (1, 0)))[:, :J]
    ha = za - 0.6 * ya1
    xtidx2g = xtu[:, idx2]
    zb = wbu.T @ xtidx2g
    hb = zb * f64(tf)[:, idx3]
    haq = mxq(ha, 0, "e4m3")
    hbq = mxq(hb, 0, "e5m2")
    a0 = haq.T @ hbq
    y = np.tanh(0.04 * a0) * f64(tv)[:, idx4]
    return y

@@ -1,0 +1,195 @@
+from contextlib import ExitStack
+
+import concourse.mybir as mybir
+
+K, T, J, I, R, C, Q = 512, 512, 256, 256, 512, 512, 512
+FLOPS = 2 * K * R * J + 2 * K * R * I + 2 * R * J * I
+
+F32 = mybir.dt.float32
+BF16 = mybir.dt.bfloat16
+I32 = mybir.dt.int32
+U32 = mybir.dt.uint32
+U16 = mybir.dt.uint16
+U8 = mybir.dt.uint8
+E4M3 = mybir.dt.float8_e4m3fn_x4
+E5M2 = mybir.dt.float8_e5m2_x4
+E2M1 = mybir.dt.float4_e2m1fn_x4
+ACT = mybir.ActivationFunctionType
+ALU = mybir.AluOpType
+
+P = 128
+SLOTS = 4
+HALF = 128
+LCOLS = HALF // 16
+
+
+def load_scale_rows(eng, plane, scales):
+    rows = scales[0].bitcast(I32)
+    for q in range(4):
+        eng.dma_start(
+            out=plane[32 * q : 32 * q + 32, :].bitcast(I32),
+            in_=rows[4 * q : 4 * q + 4, :].unsqueeze(0).to_broadcast([8, 4, 128]),
+        )
+
+
+def deal(copy, word, dst, src, run):
+    copy(
+        out=dst.bitcast(word).rearrange("p (t g w) -> p t g w", t=SLOTS, w=run),
+        in_=src.bitcast(word).rearrange("p (g t w) -> p t g w", t=SLOTS, w=run),
+    )
+
+
+def tile_list_meet_lagged_timestable_tabled_kernel(
+    tc, xt_words, xt_scales, wa_words, wa_scales, wb_words, wb_scales, tf, tv, offs, offs2, offs3, offs4, out
+):
+    nc = tc.nc
+    with ExitStack() as ctx:
+        sb = ctx.enter_context(tc.tile_pool(name="sb", bufs=1))
+        ps = ctx.enter_context(tc.psum_pool(name="ps", bufs=1))
+
+        list_a = sb.tile([P, J // 16], U16, name="list_a")
+        list_b = sb.tile([P, I // 16], U16, name="list_b")
+        list_f = sb.tile([P, I // 16], U16, name="list_f")
+        list_v = sb.tile([P, I // 16], U16, name="list_v")
+        x_w = sb.tile([P, T], U32, name="x_w", align_bytes=64)
+        x_s = sb.tile([P, T], U8, name="x_s", align_bytes=64)
+        wa_w = sb.tile([P, 2 * R], U8, name="wa_w", align_bytes=64)
+        wa_s = sb.tile([P, R], U8, name="wa_s", align_bytes=64)
+        wb_w = sb.tile([P, 4 * R], U8, name="wb_w", align_bytes=64)
+        wb_s = sb.tile([P, R], U8, name="wb_s", align_bytes=64)
+        tf_t = [sb.tile([P, C], F32, name=f"tf{t}") for t in range(SLOTS)]
+        tv_t = [sb.tile([P, Q], F32, name=f"tv{h}") for h in range(2)]
+
+        tf_rows = tf.rearrange("(g t u) c -> t g u c", t=SLOTS, u=8)
+        nc.gpsimd.dma_start(out=tf_t[0][:], in_=tf_rows[0])
+        nc.gpsimd.dma_start(out=tf_t[1][:], in_=tf_rows[1])
+        nc.sync.dma_start(out=x_w[:].bitcast(I32), in_=xt_words[0].rearrange("p c b -> p (c b)").bitcast(I32))
+        nc.sync.dma_start(list_a[:], offs)
+        load_scale_rows(nc.scalar, x_s, xt_scales)
+        nc.sync.dma_start(out=wa_w[:].bitcast(I32), in_=wa_words[0].bitcast(I32))
+        nc.sync.dma_start(list_f[:], offs3)
+        load_scale_rows(nc.sync, wa_s, wa_scales)
+        nc.sync.dma_start(list_b[:], offs2)
+        nc.sync.dma_start(out=wb_w[:].bitcast(I32), in_=wb_words[0].rearrange("p c b -> p (c b)").bitcast(I32))
+        nc.sync.dma_start(out=tf_t[2][:], in_=tf_rows[2])
+        nc.sync.dma_start(out=tf_t[3][:], in_=tf_rows[3])
+        load_scale_rows(nc.sync, wb_s, wb_scales)
+        nc.sync.dma_start(list_v[:], offs4)
+        nc.sync.dma_start(out=tv_t[0][:], in_=tv[0:P, :])
+        nc.sync.dma_start(out=tv_t[1][:], in_=tv[P : 2 * P, :])
+
+        lag = sb.tile([P, J, SLOTS], F32, name="lag")
+        first = lag[:, 0, :].bitcast(U32)
+        nc.scalar.activation(out=first, in_=first, func=ACT.Copy, scale=0.0)
+
+        xa_w = sb.tile([P, J], U32, name="xa_w", align_bytes=64)
+        xa_s = sb.tile([P, J], U8, name="xa_s", align_bytes=64)
+        xb_w = sb.tile([P, I], U32, name="xb_w", align_bytes=64)
+        xb_s = sb.tile([P, I], U8, name="xb_s", align_bytes=64)
+        wa_wd = sb.tile([P, 2 * R], U8, name="wa_wd", align_bytes=64)
+        wa_sd = sb.tile([P, R], U8, name="wa_sd", align_bytes=64)
+        wb_wd = sb.tile([P, 4 * R], U8, name="wb_wd", align_bytes=64)
+        wb_sd = sb.tile([P, R], U8, name="wb_sd", align_bytes=64)
+
+        nc.vector.tensor_copy(out=xa_w[:], in_=x_w[:].indirect(list_a[:]))
+        nc.vector.tensor_copy(out=xa_s[:], in_=x_s[:].indirect(list_a[:]))
+        deal(nc.vector.tensor_copy, I32, wa_wd[:], wa_w[:], 4)
+        deal(nc.vector.tensor_copy, I32, wa_sd[:], wa_s[:], 2)
+        nc.vector.tensor_copy(out=xb_w[:], in_=x_w[:].indirect(list_b[:]))
+        nc.vector.tensor_copy(out=xb_s[:], in_=x_s[:].indirect(list_b[:]))
+        deal(nc.vector.tensor_copy, I32, wb_wd[:], wb_w[:], 8)
+        deal(nc.scalar.copy, U32, wb_sd[:], wb_s[:], 2)
+
+        za = [ps.tile([P, SLOTS, HALF], F32, name=f"za{h}") for h in range(2)]
+        zb = [ps.tile([P, SLOTS, HALF], F32, name=f"zb{h}") for h in range(2)]
+        for h in range(2):
+            cols = slice(h * HALF, (h + 1) * HALF)
+            for t in range(SLOTS):
+                nc.tensor.matmul_mx(
+                    out=za[h][:, t, :],
+                    lhsT=wa_wd[:, 2 * P * t : 2 * P * (t + 1)].bitcast(E2M1),
+                    lhsT_scale=wa_sd[:, P * t : P * (t + 1)],
+                    rhs=xa_w[:, cols].bitcast(E4M3),
+                    rhs_scale=xa_s[:, cols],
+                    start=True,
+                    stop=True,
+                )
+        for h in range(2):
+            cols = slice(h * HALF, (h + 1) * HALF)
+            for t in range(SLOTS):
+                nc.tensor.matmul_mx(
+                    out=zb[h][:, t, :],
+                    lhsT=wb_wd[:, 4 * P * t : 4 * P * (t + 1)].bitcast(E5M2),
+                    lhsT_scale=wb_sd[:, P * t : P * (t + 1)],
+                    rhs=xb_w[:, cols].bitcast(E4M3),
+                    rhs_scale=xb_s[:, cols],
+                    start=True,
+                    stop=True,
+                )
+
+        ha = [sb.tile([P, HALF, SLOTS], BF16, name=f"ha{h}", align_bytes=64) for h in range(2)]
+        hb = [sb.tile([P, HALF, SLOTS], BF16, name=f"hb{h}", align_bytes=64) for h in range(2)]
+        ha_w = [sb.tile([P, HALF], U32, name=f"ha_w{h}", align_bytes=64) for h in range(2)]
+        ha_s = [sb.tile([P, HALF], U8, name=f"ha_s{h}", align_bytes=64) for h in range(2)]
+        hb_w = [sb.tile([P, HALF], U32, name=f"hb_w{h}", align_bytes=64) for h in range(2)]
+        hb_s = [sb.tile([P, HALF], U8, name=f"hb_s{h}", align_bytes=64) for h in range(2)]
+
+        for h in range(2):
+            n = min(HALF, J - 1 - h * HALF)
+            nc.scalar.activation(
+                out=lag[:, h * HALF + 1 : h * HALF + 1 + n, :],
+                in_=za[h][:, :, 0:n].rearrange("p t j -> p j t"),
+                func=ACT.Copy,
+                scale=-0.6,
+            )
+        for h in range(2):
+            nc.vector.tensor_tensor(
+                out=ha[h][:],
+                in0=za[h][:].rearrange("p t j -> p j t"),
+                in1=lag[:, h * HALF : (h + 1) * HALF, :],
+                op=ALU.add,
+            )
+        for h in range(2):
+            nc.vector.quantize_mx(ha_w[h][:].bitcast(E4M3), ha_s[h][:], ha[h][:].rearrange("p j t -> p (j t)"))
+
+        tf_g = [sb.tile([P, SLOTS, HALF], F32, name=f"tf_g{h}") for h in range(2)]
+        for t in range(SLOTS):
+            for h in range(2):
+                picked = tf_t[t][:].indirect(list_f[:, h * LCOLS : (h + 1) * LCOLS])
+                if t == 2:
+                    nc.vector.tensor_copy(out=tf_g[h][:, t, :], in_=picked)
+                else:
+                    nc.scalar.activation(out=tf_g[h][:, t, :], in_=picked, func=ACT.Copy)
+        tv_g = sb.tile([P, 2, I], F32, name="tv_g")
+        for g in range(2):
+            nc.scalar.activation(out=tv_g[:, g, :], in_=tv_t[g][:].indirect(list_v[:]), func=ACT.Copy)
+
+        for h in range(2):
+            nc.vector.tensor_tensor(
+                out=hb[h][:],
+                in0=zb[h][:].rearrange("p t i -> p i t"),
+                in1=tf_g[h][:].rearrange("p t i -> p i t"),
+                op=ALU.mult,
+            )
+        for h in range(2):
+            nc.vector.quantize_mx(hb_w[h][:].bitcast(E5M2), hb_s[h][:], hb[h][:].rearrange("p i t -> p (i t)"))
+
+        out_rows = out.rearrange("(g p) i -> p g i", p=P)
+        for h in range(2):
+            cols = slice(h * HALF, (h + 1) * HALF)
+            a0 = ps.tile([P, 2, HALF], F32, name=f"a0{h}")
+            for g in range(2):
+                nc.tensor.matmul_mx(
+                    out=a0[:, g, :],
+                    lhsT=ha_w[g][:].bitcast(E4M3),
+                    lhsT_scale=ha_s[g][:],
+                    rhs=hb_w[h][:].bitcast(E5M2),
+                    rhs_scale=hb_s[h][:],
+                    start=True,
+                    stop=True,
+                )
+            th = sb.tile([P, 2, HALF], F32, name=f"th{h}")
+            nc.scalar.activation(out=th[:], in_=a0[:], func=ACT.Tanh, scale=0.04)
+            y = sb.tile([P, 2, HALF], F32, name=f"y{h}")
+            nc.vector.tensor_tensor(out=y[:], in0=th[:], in1=tv_g[:, :, cols], op=ALU.mult)
+            nc.sync.dma_start(out=out_rows[:, :, cols], in_=y[:])

@@ -32,6 +32,12 @@ def load_scale_rows(eng, plane, scales):
         )
 
 
+def load_live_rows(eng, plane, scales):
+    rows = scales[0].bitcast(I32)
+    for q in range(4):
+        eng.dma_start(out=plane[32 * q : 32 * q + 4, :].bitcast(I32), in_=rows[4 * q : 4 * q + 4, :])
+
+
 def deal(copy, word, dst, src, run):
     copy(
         out=dst.bitcast(word).rearrange("p (t g w) -> p t g w", t=SLOTS, w=run),
@@ -58,25 +64,26 @@ def tile_list_meet_lagged_timestable_tabled_kernel(
         wb_w = sb.tile([P, 4 * R], U8, name="wb_w", align_bytes=64)
         wb_s = sb.tile([P, R], U8, name="wb_s", align_bytes=64)
         tf_t = [sb.tile([P, C], F32, name=f"tf{t}") for t in range(SLOTS)]
-        tv_t = [sb.tile([P, Q], F32, name=f"tv{h}") for h in range(2)]
+        tv_t = sb.tile([P, 2, Q], F32, name="tv_t")
 
+        for plane in (wa_s, wb_s):
+            nc.vector.memset(plane[:].bitcast(I32), 0)
         tf_rows = tf.rearrange("(g t u) c -> t g u c", t=SLOTS, u=8)
-        nc.gpsimd.dma_start(out=tf_t[0][:], in_=tf_rows[0])
-        nc.gpsimd.dma_start(out=tf_t[1][:], in_=tf_rows[1])
         nc.sync.dma_start(out=x_w[:].bitcast(I32), in_=xt_words[0].rearrange("p c b -> p (c b)").bitcast(I32))
         nc.sync.dma_start(list_a[:], offs)
         load_scale_rows(nc.scalar, x_s, xt_scales)
-        nc.sync.dma_start(out=wa_w[:].bitcast(I32), in_=wa_words[0].bitcast(I32))
-        nc.sync.dma_start(list_f[:], offs3)
-        load_scale_rows(nc.sync, wa_s, wa_scales)
         nc.sync.dma_start(list_b[:], offs2)
+        nc.sync.dma_start(out=wa_w[:].bitcast(I32), in_=wa_words[0].bitcast(I32))
+        load_live_rows(nc.sync, wa_s, wa_scales)
+        nc.sync.dma_start(list_f[:], offs3)
         nc.sync.dma_start(out=wb_w[:].bitcast(I32), in_=wb_words[0].rearrange("p c b -> p (c b)").bitcast(I32))
+        nc.sync.dma_start(out=tf_t[0][:], in_=tf_rows[0])
+        nc.sync.dma_start(out=tf_t[1][:], in_=tf_rows[1])
+        load_live_rows(nc.sync, wb_s, wb_scales)
         nc.sync.dma_start(out=tf_t[2][:], in_=tf_rows[2])
         nc.sync.dma_start(out=tf_t[3][:], in_=tf_rows[3])
-        load_scale_rows(nc.sync, wb_s, wb_scales)
         nc.sync.dma_start(list_v[:], offs4)
-        nc.sync.dma_start(out=tv_t[0][:], in_=tv[0:P, :])
-        nc.sync.dma_start(out=tv_t[1][:], in_=tv[P : 2 * P, :])
+        nc.sync.dma_start(out=tv_t[:], in_=tv.rearrange("(g p) q -> p g q", p=P))
 
         lag = sb.tile([P, J, SLOTS], F32, name="lag")
         first = lag[:, 0, :].bitcast(U32)
@@ -93,7 +100,7 @@ def tile_list_meet_lagged_timestable_tabled_kernel(
 
         nc.vector.tensor_copy(out=xa_w[:], in_=x_w[:].indirect(list_a[:]))
         nc.vector.tensor_copy(out=xa_s[:], in_=x_s[:].indirect(list_a[:]))
-        deal(nc.vector.tensor_copy, I32, wa_wd[:], wa_w[:], 4)
+        deal(nc.scalar.copy, U32, wa_wd[:], wa_w[:], 4)
         deal(nc.vector.tensor_copy, I32, wa_sd[:], wa_s[:], 2)
         nc.vector.tensor_copy(out=xb_w[:], in_=x_w[:].indirect(list_b[:]))
         nc.vector.tensor_copy(out=xb_s[:], in_=x_s[:].indirect(list_b[:]))
@@ -127,10 +134,10 @@ def tile_list_meet_lagged_timestable_tabled_kernel(
                     stop=True,
                 )
 
-        ha = [sb.tile([P, HALF, SLOTS], BF16, name=f"ha{h}", align_bytes=64) for h in range(2)]
+        ha = sb.tile([P, J, SLOTS], BF16, name="ha", align_bytes=64)
         hb = [sb.tile([P, HALF, SLOTS], BF16, name=f"hb{h}", align_bytes=64) for h in range(2)]
-        ha_w = [sb.tile([P, HALF], U32, name=f"ha_w{h}", align_bytes=64) for h in range(2)]
-        ha_s = [sb.tile([P, HALF], U8, name=f"ha_s{h}", align_bytes=64) for h in range(2)]
+        ha_w = sb.tile([P, J], U32, name="ha_w", align_bytes=64)
+        ha_s = sb.tile([P, J], U8, name="ha_s", align_bytes=64)
         hb_w = [sb.tile([P, HALF], U32, name=f"hb_w{h}", align_bytes=64) for h in range(2)]
         hb_s = [sb.tile([P, HALF], U8, name=f"hb_s{h}", align_bytes=64) for h in range(2)]
 
@@ -144,52 +151,51 @@ def tile_list_meet_lagged_timestable_tabled_kernel(
             )
         for h in range(2):
             nc.vector.tensor_tensor(
-                out=ha[h][:],
+                out=ha[:, h * HALF : (h + 1) * HALF, :],
                 in0=za[h][:].rearrange("p t j -> p j t"),
                 in1=lag[:, h * HALF : (h + 1) * HALF, :],
                 op=ALU.add,
             )
-        for h in range(2):
-            nc.vector.quantize_mx(ha_w[h][:].bitcast(E4M3), ha_s[h][:], ha[h][:].rearrange("p j t -> p (j t)"))
+        nc.vector.quantize_mx(ha_w[:].bitcast(E4M3), ha_s[:], ha[:].rearrange("p j t -> p (j t)"))
 
         tf_g = [sb.tile([P, SLOTS, HALF], F32, name=f"tf_g{h}") for h in range(2)]
-        for t in range(SLOTS):
-            for h in range(2):
+        for h in range(2):
+            for t in range(SLOTS):
                 picked = tf_t[t][:].indirect(list_f[:, h * LCOLS : (h + 1) * LCOLS])
-                if t == 2:
+                if t == 0:
                     nc.vector.tensor_copy(out=tf_g[h][:, t, :], in_=picked)
                 else:
                     nc.scalar.activation(out=tf_g[h][:, t, :], in_=picked, func=ACT.Copy)
         tv_g = sb.tile([P, 2, I], F32, name="tv_g")
         for g in range(2):
-            nc.scalar.activation(out=tv_g[:, g, :], in_=tv_t[g][:].indirect(list_v[:]), func=ACT.Copy)
+            nc.scalar.activation(out=tv_g[:, g, :], in_=tv_t[:, g, :].indirect(list_v[:]), func=ACT.Copy)
 
         for h in range(2):
             nc.vector.tensor_tensor(
-                out=hb[h][:],
-                in0=zb[h][:].rearrange("p t i -> p i t"),
-                in1=tf_g[h][:].rearrange("p t i -> p i t"),
+                out=hb[h][:].rearrange("p (i e) t -> p i t e", e=2),
+                in0=zb[h][:].rearrange("p t (i e) -> p i t e", e=2),
+                in1=tf_g[h][:].rearrange("p t (i e) -> p i t e", e=2),
                 op=ALU.mult,
             )
         for h in range(2):
             nc.vector.quantize_mx(hb_w[h][:].bitcast(E5M2), hb_s[h][:], hb[h][:].rearrange("p i t -> p (i t)"))
 
-        out_rows = out.rearrange("(g p) i -> p g i", p=P)
         for h in range(2):
             cols = slice(h * HALF, (h + 1) * HALF)
-            a0 = ps.tile([P, 2, HALF], F32, name=f"a0{h}")
             for g in range(2):
+                rows = slice(g * P, (g + 1) * P)
+                a0 = ps.tile([P, HALF], F32, name=f"a0{h}{g}")
                 nc.tensor.matmul_mx(
-                    out=a0[:, g, :],
-                    lhsT=ha_w[g][:].bitcast(E4M3),
-                    lhsT_scale=ha_s[g][:],
+                    out=a0[:],
+                    lhsT=ha_w[:, rows].bitcast(E4M3),
+                    lhsT_scale=ha_s[:, rows],
                     rhs=hb_w[h][:].bitcast(E5M2),
                     rhs_scale=hb_s[h][:],
                     start=True,
                     stop=True,
                 )
-            th = sb.tile([P, 2, HALF], F32, name=f"th{h}")
-            nc.scalar.activation(out=th[:], in_=a0[:], func=ACT.Tanh, scale=0.04)
-            y = sb.tile([P, 2, HALF], F32, name=f"y{h}")
-            nc.vector.tensor_tensor(out=y[:], in0=th[:], in1=tv_g[:, :, cols], op=ALU.mult)
-            nc.sync.dma_start(out=out_rows[:, :, cols], in_=y[:])
+                th = sb.tile([P, HALF], F32, name=f"th{h}{g}")
+                nc.scalar.activation(out=th[:], in_=a0[:], func=ACT.Tanh, scale=0.04)
+                y = sb.tile([P, HALF], F32, name=f"y{h}{g}")
+                nc.vector.tensor_tensor(out=y[:], in0=th[:], in1=tv_g[:, g, cols], op=ALU.mult)
+                nc.sync.dma_start(out=out[rows, cols], in_=y[:])

@@ -20,16 +20,6 @@ ALU = mybir.AluOpType
 P = 128
 SLOTS = 4
 HALF = 128
-LCOLS = HALF // 16
-
-
-def load_scale_rows(eng, plane, scales):
-    rows = scales[0].bitcast(I32)
-    for q in range(4):
-        eng.dma_start(
-            out=plane[32 * q : 32 * q + 32, :].bitcast(I32),
-            in_=rows[4 * q : 4 * q + 4, :].unsqueeze(0).to_broadcast([8, 4, 128]),
-        )
 
 
 def load_live_rows(eng, plane, scales):
@@ -64,29 +54,30 @@ def tile_list_meet_lagged_timestable_tabled_kernel(
         wb_w = sb.tile([P, 4 * R], U8, name="wb_w", align_bytes=64)
         wb_s = sb.tile([P, R], U8, name="wb_s", align_bytes=64)
         tf_t = [sb.tile([P, C], F32, name=f"tf{t}") for t in range(SLOTS)]
-        tv_t = sb.tile([P, 2, Q], F32, name="tv_t")
+        tv_t = [sb.tile([P, Q], F32, name=f"tv{h}") for h in range(2)]
 
-        for plane in (wa_s, wb_s):
+        for plane in (x_s, wa_s, wb_s):
             nc.vector.memset(plane[:].bitcast(I32), 0)
         tf_rows = tf.rearrange("(g t u) c -> t g u c", t=SLOTS, u=8)
-        nc.sync.dma_start(out=x_w[:].bitcast(I32), in_=xt_words[0].rearrange("p c b -> p (c b)").bitcast(I32))
         nc.sync.dma_start(list_a[:], offs)
-        load_scale_rows(nc.scalar, x_s, xt_scales)
         nc.sync.dma_start(list_b[:], offs2)
+        load_live_rows(nc.sync, x_s, xt_scales)
+        nc.sync.dma_start(out=x_w[:].bitcast(I32), in_=xt_words[0].rearrange("p c b -> p (c b)").bitcast(I32))
         nc.sync.dma_start(out=wa_w[:].bitcast(I32), in_=wa_words[0].bitcast(I32))
         load_live_rows(nc.sync, wa_s, wa_scales)
         nc.sync.dma_start(list_f[:], offs3)
-        nc.sync.dma_start(out=wb_w[:].bitcast(I32), in_=wb_words[0].rearrange("p c b -> p (c b)").bitcast(I32))
         nc.sync.dma_start(out=tf_t[0][:], in_=tf_rows[0])
+        nc.sync.dma_start(out=wb_w[:].bitcast(I32), in_=wb_words[0].rearrange("p c b -> p (c b)").bitcast(I32))
         nc.sync.dma_start(out=tf_t[1][:], in_=tf_rows[1])
         load_live_rows(nc.sync, wb_s, wb_scales)
         nc.sync.dma_start(out=tf_t[2][:], in_=tf_rows[2])
         nc.sync.dma_start(out=tf_t[3][:], in_=tf_rows[3])
         nc.sync.dma_start(list_v[:], offs4)
-        nc.sync.dma_start(out=tv_t[:], in_=tv.rearrange("(g p) q -> p g q", p=P))
+        for g in range(2):
+            nc.sync.dma_start(out=tv_t[g][:], in_=tv[g * P : (g + 1) * P, :])
 
-        lag = sb.tile([P, J, SLOTS], F32, name="lag")
-        first = lag[:, 0, :].bitcast(U32)
+        lag = sb.tile([P, J * SLOTS], F32, name="lag")
+        first = lag[:, 0:SLOTS].bitcast(U32)
         nc.scalar.activation(out=first, in_=first, func=ACT.Copy, scale=0.0)
 
         xa_w = sb.tile([P, J], U32, name="xa_w", align_bytes=64)
@@ -98,14 +89,14 @@ def tile_list_meet_lagged_timestable_tabled_kernel(
         wb_wd = sb.tile([P, 4 * R], U8, name="wb_wd", align_bytes=64)
         wb_sd = sb.tile([P, R], U8, name="wb_sd", align_bytes=64)
 
-        nc.vector.tensor_copy(out=xa_w[:], in_=x_w[:].indirect(list_a[:]))
         nc.vector.tensor_copy(out=xa_s[:], in_=x_s[:].indirect(list_a[:]))
-        deal(nc.scalar.copy, U32, wa_wd[:], wa_w[:], 4)
-        deal(nc.vector.tensor_copy, I32, wa_sd[:], wa_s[:], 2)
-        nc.vector.tensor_copy(out=xb_w[:], in_=x_w[:].indirect(list_b[:]))
         nc.vector.tensor_copy(out=xb_s[:], in_=x_s[:].indirect(list_b[:]))
+        nc.vector.tensor_copy(out=xa_w[:], in_=x_w[:].indirect(list_a[:]))
+        nc.vector.tensor_copy(out=xb_w[:], in_=x_w[:].indirect(list_b[:]))
+        deal(nc.scalar.copy, U32, wa_wd[:], wa_w[:], 4)
+        deal(nc.scalar.copy, U32, wa_sd[:], wa_s[:], 2)
         deal(nc.vector.tensor_copy, I32, wb_wd[:], wb_w[:], 8)
-        deal(nc.scalar.copy, U32, wb_sd[:], wb_s[:], 2)
+        deal(nc.gpsimd.tensor_copy, I32, wb_sd[:], wb_s[:], 2)
 
         za = [ps.tile([P, SLOTS, HALF], F32, name=f"za{h}") for h in range(2)]
         zb = [ps.tile([P, SLOTS, HALF], F32, name=f"zb{h}") for h in range(2)]
@@ -143,8 +134,9 @@ def tile_list_meet_lagged_timestable_tabled_kernel(
 
         for h in range(2):
             n = min(HALF, J - 1 - h * HALF)
+            c0 = (h * HALF + 1) * SLOTS
             nc.scalar.activation(
-                out=lag[:, h * HALF + 1 : h * HALF + 1 + n, :],
+                out=lag[:, c0 : c0 + n * SLOTS].rearrange("p (j t) -> p j t", t=SLOTS),
                 in_=za[h][:, :, 0:n].rearrange("p t j -> p j t"),
                 func=ACT.Copy,
                 scale=-0.6,
@@ -153,33 +145,33 @@ def tile_list_meet_lagged_timestable_tabled_kernel(
             nc.vector.tensor_tensor(
                 out=ha[:, h * HALF : (h + 1) * HALF, :],
                 in0=za[h][:].rearrange("p t j -> p j t"),
-                in1=lag[:, h * HALF : (h + 1) * HALF, :],
+                in1=lag[:, h * HALF * SLOTS : (h + 1) * HALF * SLOTS].rearrange("p (j t) -> p j t", t=SLOTS),
                 op=ALU.add,
             )
         nc.vector.quantize_mx(ha_w[:].bitcast(E4M3), ha_s[:], ha[:].rearrange("p j t -> p (j t)"))
 
-        tf_g = [sb.tile([P, SLOTS, HALF], F32, name=f"tf_g{h}") for h in range(2)]
-        for h in range(2):
-            for t in range(SLOTS):
-                picked = tf_t[t][:].indirect(list_f[:, h * LCOLS : (h + 1) * LCOLS])
-                if t == 0:
-                    nc.vector.tensor_copy(out=tf_g[h][:, t, :], in_=picked)
-                else:
-                    nc.scalar.activation(out=tf_g[h][:, t, :], in_=picked, func=ACT.Copy)
+        tf_g = sb.tile([P, SLOTS, I], F32, name="tf_g")
+        for t in range(SLOTS):
+            picked = tf_t[t][:].indirect(list_f[:])
+            if t in (0, SLOTS - 1):
+                nc.vector.tensor_copy(out=tf_g[:, t, :], in_=picked)
+            else:
+                nc.scalar.activation(out=tf_g[:, t, :], in_=picked, func=ACT.Copy)
         tv_g = sb.tile([P, 2, I], F32, name="tv_g")
         for g in range(2):
-            nc.scalar.activation(out=tv_g[:, g, :], in_=tv_t[:, g, :].indirect(list_v[:]), func=ACT.Copy)
+            nc.scalar.activation(out=tv_g[:, g, :], in_=tv_t[g][:].indirect(list_v[:]), func=ACT.Copy)
 
         for h in range(2):
             nc.vector.tensor_tensor(
                 out=hb[h][:].rearrange("p (i e) t -> p i t e", e=2),
                 in0=zb[h][:].rearrange("p t (i e) -> p i t e", e=2),
-                in1=tf_g[h][:].rearrange("p t (i e) -> p i t e", e=2),
+                in1=tf_g[:, :, h * HALF : (h + 1) * HALF].rearrange("p t (i e) -> p i t e", e=2),
                 op=ALU.mult,
             )
         for h in range(2):
             nc.vector.quantize_mx(hb_w[h][:].bitcast(E5M2), hb_s[h][:], hb[h][:].rearrange("p i t -> p (i t)"))
 
+        th = sb.tile([P, 2, 2, HALF], F32, name="th", tag="tv1")
         for h in range(2):
             cols = slice(h * HALF, (h + 1) * HALF)
             for g in range(2):
@@ -194,8 +186,7 @@ def tile_list_meet_lagged_timestable_tabled_kernel(
                     start=True,
                     stop=True,
                 )
-                th = sb.tile([P, HALF], F32, name=f"th{h}{g}")
-                nc.scalar.activation(out=th[:], in_=a0[:], func=ACT.Tanh, scale=0.04)
+                nc.scalar.activation(out=th[:, h, g, :], in_=a0[:], func=ACT.Tanh, scale=0.04)
                 y = sb.tile([P, HALF], F32, name=f"y{h}{g}")
-                nc.vector.tensor_tensor(out=y[:], in0=th[:], in1=tv_g[:, g, cols], op=ALU.mult)
+                nc.vector.tensor_tensor(out=y[:], in0=th[:, h, g, :], in1=tv_g[:, g, cols], op=ALU.mult)
                 nc.sync.dma_start(out=out[rows, cols], in_=y[:])

@@ -67,8 +67,8 @@ def tile_list_meet_lagged_timestable_tabled_kernel(
         load_live_rows(nc.sync, wa_s, wa_scales)
         nc.sync.dma_start(list_f[:], offs3)
         nc.sync.dma_start(out=tf_t[0][:], in_=tf_rows[0])
-        nc.sync.dma_start(out=wb_w[:].bitcast(I32), in_=wb_words[0].rearrange("p c b -> p (c b)").bitcast(I32))
         nc.sync.dma_start(out=tf_t[1][:], in_=tf_rows[1])
+        nc.sync.dma_start(out=wb_w[:].bitcast(I32), in_=wb_words[0].rearrange("p c b -> p (c b)").bitcast(I32))
         load_live_rows(nc.sync, wb_s, wb_scales)
         nc.sync.dma_start(out=tf_t[2][:], in_=tf_rows[2])
         nc.sync.dma_start(out=tf_t[3][:], in_=tf_rows[3])
@@ -95,8 +95,6 @@ def tile_list_meet_lagged_timestable_tabled_kernel(
         nc.vector.tensor_copy(out=xb_w[:], in_=x_w[:].indirect(list_b[:]))
         deal(nc.scalar.copy, U32, wa_wd[:], wa_w[:], 4)
         deal(nc.scalar.copy, U32, wa_sd[:], wa_s[:], 2)
-        deal(nc.vector.tensor_copy, I32, wb_wd[:], wb_w[:], 8)
-        deal(nc.gpsimd.tensor_copy, I32, wb_sd[:], wb_s[:], 2)
 
         za = [ps.tile([P, SLOTS, HALF], F32, name=f"za{h}") for h in range(2)]
         zb = [ps.tile([P, SLOTS, HALF], F32, name=f"zb{h}") for h in range(2)]
@@ -109,18 +107,6 @@ def tile_list_meet_lagged_timestable_tabled_kernel(
                     lhsT_scale=wa_sd[:, P * t : P * (t + 1)],
                     rhs=xa_w[:, cols].bitcast(E4M3),
                     rhs_scale=xa_s[:, cols],
-                    start=True,
-                    stop=True,
-                )
-        for h in range(2):
-            cols = slice(h * HALF, (h + 1) * HALF)
-            for t in range(SLOTS):
-                nc.tensor.matmul_mx(
-                    out=zb[h][:, t, :],
-                    lhsT=wb_wd[:, 4 * P * t : 4 * P * (t + 1)].bitcast(E5M2),
-                    lhsT_scale=wb_sd[:, P * t : P * (t + 1)],
-                    rhs=xb_w[:, cols].bitcast(E4M3),
-                    rhs_scale=xb_s[:, cols],
                     start=True,
                     stop=True,
                 )
@@ -150,26 +136,47 @@ def tile_list_meet_lagged_timestable_tabled_kernel(
             )
         nc.vector.quantize_mx(ha_w[:].bitcast(E4M3), ha_s[:], ha[:].rearrange("p j t -> p (j t)"))
 
+        deal(nc.scalar.copy, U32, wb_wd[:], wb_w[:], 8)
+        deal(nc.gpsimd.tensor_copy, I32, wb_sd[:], wb_s[:], 2)
+        for h in range(2):
+            cols = slice(h * HALF, (h + 1) * HALF)
+            for t in range(SLOTS):
+                nc.tensor.matmul_mx(
+                    out=zb[h][:, t, :],
+                    lhsT=wb_wd[:, 4 * P * t : 4 * P * (t + 1)].bitcast(E5M2),
+                    lhsT_scale=wb_sd[:, P * t : P * (t + 1)],
+                    rhs=xb_w[:, cols].bitcast(E4M3),
+                    rhs_scale=xb_s[:, cols],
+                    start=True,
+                    stop=True,
+                )
+
         tf_g = sb.tile([P, SLOTS, I], F32, name="tf_g")
-        for t in range(SLOTS):
-            picked = tf_t[t][:].indirect(list_f[:])
-            if t in (0, SLOTS - 1):
-                nc.vector.tensor_copy(out=tf_g[:, t, :], in_=picked)
-            else:
-                nc.scalar.activation(out=tf_g[:, t, :], in_=picked, func=ACT.Copy)
+        for t in range(2):
+            nc.vector.tensor_copy(out=tf_g[:, t, :], in_=tf_t[t][:].indirect(list_f[:]))
+        nc.scalar.activation(out=tf_g[:, 2, :], in_=tf_t[2][:].indirect(list_f[:]), func=ACT.Copy)
+        nc.scalar.activation(out=tf_g[:, 3, :HALF], in_=tf_t[3][:].indirect(list_f[:, : HALF // 16]), func=ACT.Copy)
+        nc.vector.tensor_copy(out=tf_g[:, 3, HALF:], in_=tf_t[3][:].indirect(list_f[:, HALF // 16 :]))
         tv_g = sb.tile([P, 2, I], F32, name="tv_g")
         for g in range(2):
             nc.scalar.activation(out=tv_g[:, g, :], in_=tv_t[g][:].indirect(list_v[:]), func=ACT.Copy)
 
-        for h in range(2):
+        def times_factors(h, c0, c1):
             nc.vector.tensor_tensor(
-                out=hb[h][:].rearrange("p (i e) t -> p i t e", e=2),
-                in0=zb[h][:].rearrange("p t (i e) -> p i t e", e=2),
-                in1=tf_g[:, :, h * HALF : (h + 1) * HALF].rearrange("p t (i e) -> p i t e", e=2),
+                out=hb[h][:, c0:c1, :].rearrange("p (i e) t -> p i t e", e=2),
+                in0=zb[h][:, :, c0:c1].rearrange("p t (i e) -> p i t e", e=2),
+                in1=tf_g[:, :, h * HALF + c0 : h * HALF + c1].rearrange("p t (i e) -> p i t e", e=2),
                 op=ALU.mult,
             )
-        for h in range(2):
+
+        def quantise_hb(h):
             nc.vector.quantize_mx(hb_w[h][:].bitcast(E5M2), hb_s[h][:], hb[h][:].rearrange("p i t -> p (i t)"))
+
+        times_factors(0, 0, HALF)
+        times_factors(1, 0, HALF // 2)
+        quantise_hb(0)
+        times_factors(1, HALF // 2, HALF)
+        quantise_hb(1)
 
         th = sb.tile([P, 2, 2, HALF], F32, name="th", tag="tv1")
         for h in range(2):

from contextlib import ExitStack

import concourse.mybir as mybir

K, T, J, I, R, C, Q = 512, 512, 256, 256, 512, 512, 512
FLOPS = 2 * K * R * J + 2 * K * R * I + 2 * R * J * I

F32 = mybir.dt.float32
BF16 = mybir.dt.bfloat16
I32 = mybir.dt.int32
U32 = mybir.dt.uint32
U16 = mybir.dt.uint16
U8 = mybir.dt.uint8
E4M3 = mybir.dt.float8_e4m3fn_x4
E5M2 = mybir.dt.float8_e5m2_x4
E2M1 = mybir.dt.float4_e2m1fn_x4
ACT = mybir.ActivationFunctionType
ALU = mybir.AluOpType

P = 128
SLOTS = 4
HALF = 128


def load_live_rows(eng, plane, scales):
    rows = scales[0].bitcast(I32)
    for q in range(4):
        eng.dma_start(out=plane[32 * q : 32 * q + 4, :].bitcast(I32), in_=rows[4 * q : 4 * q + 4, :])


def deal(copy, word, dst, src, run):
    copy(
        out=dst.bitcast(word).rearrange("p (t g w) -> p t g w", t=SLOTS, w=run),
        in_=src.bitcast(word).rearrange("p (g t w) -> p t g w", t=SLOTS, w=run),
    )


def tile_list_meet_lagged_timestable_tabled_kernel(
    tc, xt_words, xt_scales, wa_words, wa_scales, wb_words, wb_scales, tf, tv, offs, offs2, offs3, offs4, out
):
    nc = tc.nc
    with ExitStack() as ctx:
        sb = ctx.enter_context(tc.tile_pool(name="sb", bufs=1))
        ps = ctx.enter_context(tc.psum_pool(name="ps", bufs=1))

        list_a = sb.tile([P, J // 16], U16, name="list_a")
        list_b = sb.tile([P, I // 16], U16, name="list_b")
        list_f = sb.tile([P, I // 16], U16, name="list_f")
        list_v = sb.tile([P, I // 16], U16, name="list_v")
        x_w = sb.tile([P, T], U32, name="x_w", align_bytes=64)
        x_s = sb.tile([P, T], U8, name="x_s", align_bytes=64)
        wa_w = sb.tile([P, 2 * R], U8, name="wa_w", align_bytes=64)
        wa_s = sb.tile([P, R], U8, name="wa_s", align_bytes=64)
        wb_w = sb.tile([P, 4 * R], U8, name="wb_w", align_bytes=64)
        wb_s = sb.tile([P, R], U8, name="wb_s", align_bytes=64)
        tf_t = [sb.tile([P, C], F32, name=f"tf{t}") for t in range(SLOTS)]
        tv_t = [sb.tile([P, Q], F32, name=f"tv{h}") for h in range(2)]

        for plane in (x_s, wa_s, wb_s):
            nc.vector.memset(plane[:].bitcast(I32), 0)
        tf_rows = tf.rearrange("(g t u) c -> t g u c", t=SLOTS, u=8)
        nc.sync.dma_start(list_a[:], offs)
        nc.sync.dma_start(list_b[:], offs2)
        load_live_rows(nc.sync, x_s, xt_scales)
        nc.sync.dma_start(out=x_w[:].bitcast(I32), in_=xt_words[0].rearrange("p c b -> p (c b)").bitcast(I32))
        nc.sync.dma_start(out=wa_w[:].bitcast(I32), in_=wa_words[0].bitcast(I32))
        load_live_rows(nc.sync, wa_s, wa_scales)
        nc.sync.dma_start(list_f[:], offs3)
        nc.sync.dma_start(out=tf_t[0][:], in_=tf_rows[0])
        nc.sync.dma_start(out=tf_t[1][:], in_=tf_rows[1])
        nc.sync.dma_start(out=wb_w[:].bitcast(I32), in_=wb_words[0].rearrange("p c b -> p (c b)").bitcast(I32))
        load_live_rows(nc.sync, wb_s, wb_scales)
        nc.sync.dma_start(out=tf_t[2][:], in_=tf_rows[2])
        nc.sync.dma_start(out=tf_t[3][:], in_=tf_rows[3])
        nc.sync.dma_start(list_v[:], offs4)
        for g in range(2):
            nc.sync.dma_start(out=tv_t[g][:], in_=tv[g * P : (g + 1) * P, :])

        lag = sb.tile([P, J * SLOTS], F32, name="lag")
        first = lag[:, 0:SLOTS].bitcast(U32)
        nc.scalar.activation(out=first, in_=first, func=ACT.Copy, scale=0.0)

        xa_w = sb.tile([P, J], U32, name="xa_w", align_bytes=64)
        xa_s = sb.tile([P, J], U8, name="xa_s", align_bytes=64)
        xb_w = sb.tile([P, I], U32, name="xb_w", align_bytes=64)
        xb_s = sb.tile([P, I], U8, name="xb_s", align_bytes=64)
        wa_wd = sb.tile([P, 2 * R], U8, name="wa_wd", align_bytes=64)
        wa_sd = sb.tile([P, R], U8, name="wa_sd", align_bytes=64)
        wb_wd = sb.tile([P, 4 * R], U8, name="wb_wd", align_bytes=64)
        wb_sd = sb.tile([P, R], U8, name="wb_sd", align_bytes=64)

        nc.vector.tensor_copy(out=xa_s[:], in_=x_s[:].indirect(list_a[:]))
        nc.vector.tensor_copy(out=xb_s[:], in_=x_s[:].indirect(list_b[:]))
        nc.vector.tensor_copy(out=xa_w[:], in_=x_w[:].indirect(list_a[:]))
        nc.vector.tensor_copy(out=xb_w[:], in_=x_w[:].indirect(list_b[:]))
        deal(nc.scalar.copy, U32, wa_wd[:], wa_w[:], 4)
        deal(nc.scalar.copy, U32, wa_sd[:], wa_s[:], 2)

        za = [ps.tile([P, SLOTS, HALF], F32, name=f"za{h}") for h in range(2)]
        zb = [ps.tile([P, SLOTS, HALF], F32, name=f"zb{h}") for h in range(2)]
        for h in range(2):
            cols = slice(h * HALF, (h + 1) * HALF)
            for t in range(SLOTS):
                nc.tensor.matmul_mx(
                    out=za[h][:, t, :],
                    lhsT=wa_wd[:, 2 * P * t : 2 * P * (t + 1)].bitcast(E2M1),
                    lhsT_scale=wa_sd[:, P * t : P * (t + 1)],
                    rhs=xa_w[:, cols].bitcast(E4M3),
                    rhs_scale=xa_s[:, cols],
                    start=True,
                    stop=True,
                )

        ha = sb.tile([P, J, SLOTS], BF16, name="ha", align_bytes=64)
        hb = [sb.tile([P, HALF, SLOTS], BF16, name=f"hb{h}", align_bytes=64) for h in range(2)]
        ha_w = sb.tile([P, J], U32, name="ha_w", align_bytes=64)
        ha_s = sb.tile([P, J], U8, name="ha_s", align_bytes=64)
        hb_w = [sb.tile([P, HALF], U32, name=f"hb_w{h}", align_bytes=64) for h in range(2)]
        hb_s = [sb.tile([P, HALF], U8, name=f"hb_s{h}", align_bytes=64) for h in range(2)]

        for h in range(2):
            n = min(HALF, J - 1 - h * HALF)
            c0 = (h * HALF + 1) * SLOTS
            nc.scalar.activation(
                out=lag[:, c0 : c0 + n * SLOTS].rearrange("p (j t) -> p j t", t=SLOTS),
                in_=za[h][:, :, 0:n].rearrange("p t j -> p j t"),
                func=ACT.Copy,
                scale=-0.6,
            )
        for h in range(2):
            nc.vector.tensor_tensor(
                out=ha[:, h * HALF : (h + 1) * HALF, :],
                in0=za[h][:].rearrange("p t j -> p j t"),
                in1=lag[:, h * HALF * SLOTS : (h + 1) * HALF * SLOTS].rearrange("p (j t) -> p j t", t=SLOTS),
                op=ALU.add,
            )
        nc.vector.quantize_mx(ha_w[:].bitcast(E4M3), ha_s[:], ha[:].rearrange("p j t -> p (j t)"))

        deal(nc.scalar.copy, U32, wb_wd[:], wb_w[:], 8)
        deal(nc.gpsimd.tensor_copy, I32, wb_sd[:], wb_s[:], 2)
        for h in range(2):
            cols = slice(h * HALF, (h + 1) * HALF)
            for t in range(SLOTS):
                nc.tensor.matmul_mx(
                    out=zb[h][:, t, :],
                    lhsT=wb_wd[:, 4 * P * t : 4 * P * (t + 1)].bitcast(E5M2),
                    lhsT_scale=wb_sd[:, P * t : P * (t + 1)],
                    rhs=xb_w[:, cols].bitcast(E4M3),
                    rhs_scale=xb_s[:, cols],
                    start=True,
                    stop=True,
                )

        tf_g = sb.tile([P, SLOTS, I], F32, name="tf_g")
        for t in range(2):
            nc.vector.tensor_copy(out=tf_g[:, t, :], in_=tf_t[t][:].indirect(list_f[:]))
        nc.scalar.activation(out=tf_g[:, 2, :], in_=tf_t[2][:].indirect(list_f[:]), func=ACT.Copy)
        nc.scalar.activation(out=tf_g[:, 3, :HALF], in_=tf_t[3][:].indirect(list_f[:, : HALF // 16]), func=ACT.Copy)
        nc.vector.tensor_copy(out=tf_g[:, 3, HALF:], in_=tf_t[3][:].indirect(list_f[:, HALF // 16 :]))
        tv_g = sb.tile([P, 2, I], F32, name="tv_g")
        for g in range(2):
            nc.scalar.activation(out=tv_g[:, g, :], in_=tv_t[g][:].indirect(list_v[:]), func=ACT.Copy)

        def times_factors(h, c0, c1):
            nc.vector.tensor_tensor(
                out=hb[h][:, c0:c1, :].rearrange("p (i e) t -> p i t e", e=2),
                in0=zb[h][:, :, c0:c1].rearrange("p t (i e) -> p i t e", e=2),
                in1=tf_g[:, :, h * HALF + c0 : h * HALF + c1].rearrange("p t (i e) -> p i t e", e=2),
                op=ALU.mult,
            )

        def quantise_hb(h):
            nc.vector.quantize_mx(hb_w[h][:].bitcast(E5M2), hb_s[h][:], hb[h][:].rearrange("p i t -> p (i t)"))

        times_factors(0, 0, HALF)
        times_factors(1, 0, HALF // 2)
        quantise_hb(0)
        times_factors(1, HALF // 2, HALF)
        quantise_hb(1)

        th = sb.tile([P, 2, 2, HALF], F32, name="th", tag="tv1")
        for h in range(2):
            cols = slice(h * HALF, (h + 1) * HALF)
            for g in range(2):
                rows = slice(g * P, (g + 1) * P)
                a0 = ps.tile([P, HALF], F32, name=f"a0{h}{g}")
                nc.tensor.matmul_mx(
                    out=a0[:],
                    lhsT=ha_w[:, rows].bitcast(E4M3),
                    lhsT_scale=ha_s[:, rows],
                    rhs=hb_w[h][:].bitcast(E5M2),
                    rhs_scale=hb_s[h][:],
                    start=True,
                    stop=True,
                )
                nc.scalar.activation(out=th[:, h, g, :], in_=a0[:], func=ACT.Tanh, scale=0.04)
                y = sb.tile([P, HALF], F32, name=f"y{h}{g}")
                nc.vector.tensor_tensor(out=y[:], in0=th[:, h, g, :], in1=tv_g[:, g, cols], op=ALU.mult)
                nc.sync.dma_start(out=out[rows, cols], in_=y[:])
